import numpy as np
import ml_dtypes


def mxq(x, axis, fmt="e4m3"):
    dtype, down = {"e4m3": (ml_dtypes.float8_e4m3fn, 7), "e5m2": (ml_dtypes.float8_e5m2, 14)}[fmt]
    v = np.moveaxis(np.asarray(x, np.float32).astype(ml_dtypes.bfloat16).astype(np.float64), axis, -1)
    blocks = v.reshape(v.shape[:-1] + (-1, 32))
    amax = np.abs(blocks).max(-1, keepdims=True)
    byte = np.maximum(np.where(amax > 0, np.frexp(amax)[1] - 1 + 127, 0) - down, 1)
    scale = np.exp2(byte - 127.0)
    codes = (blocks / scale).astype(np.float32).astype(dtype).astype(np.float64)
    return np.moveaxis((codes * scale).reshape(v.shape), -1, axis)


WIDE = False


def mx_kscale(k, group=512):
    if not WIDE:
        return np.ones(k)
    levels = np.array([18, -18])
    if group != 512:
        return np.exp2(np.random.permutation(np.resize(levels, k // group))).repeat(group)
    if k % 512:
        return np.exp2(np.random.permutation(np.resize(levels, k // 32))).repeat(32)
    a = np.empty((k // 512, 16))
    for p in range(k // 512):
        a[p, :8] = np.random.permutation(np.resize(levels, 8))
        for g in range(8):
            far = levels[np.abs(levels - a[p, g]) >= 10]
            a[p, g + 8] = far[np.random.randint(len(far))]
    return np.exp2(a.ravel()).repeat(32)


def f64(x):
    return np.asarray(x).astype(np.float64)


E2M1 = np.array([0.0, 0.5, 1.0, 1.5, 2.0, 3.0, 4.0, 6.0, -0.0, -0.5, -1.0, -1.5, -2.0, -3.0, -4.0, -6.0])


def pack_group(w):
    k, n = w.shape
    w = f64(np.asarray(w, np.float32).astype(ml_dtypes.bfloat16)).reshape(k // 32, 32, n)
    amax = np.abs(w).max(1)
    mant, ex = np.frexp(amax / 6.0)
    byte = np.clip(np.where(amax > 0, np.where(mant > 0.5, ex, ex - 1) + 127, 1), 1, 254)
    scaled = (w * np.exp2(127.0 - byte)[:, None, :]).reshape(k, n).astype(np.float32)
    c = np.ascontiguousarray(scaled.reshape(k // 4, 4, n).transpose(0, 2, 1)).astype(ml_dtypes.float4_e2m1fn).view(np.uint8) & 0xF
    return np.ascontiguousarray((c[..., 0::2] | (c[..., 1::2] << 4)).reshape(k // 4, 2 * n)), byte.astype(np.uint8)


def unpack_group(words, scales):
    p, n = words.shape[0], scales.shape[1]
    words = np.ascontiguousarray(words).reshape(p, n, 2)
    nib = np.empty((p, n, 4), np.uint8)
    nib[..., 0::2] = words & 0xF
    nib[..., 1::2] = words >> 4
    return E2M1[nib].transpose(0, 2, 1).reshape(4 * p, n) * np.repeat(np.exp2(scales.astype(np.float64) - 127.0), 32, axis=0)


def sigmoid(v):
    return 1.0 / (1.0 + np.exp(-v))


G, D, M, N = 4, 128, 128, 512


def setup_inputs():
    n = np.random.standard_normal
    s_d = mx_kscale(D, 0)
    wi_ = [pack_group(w) for w in n((G, D, M)) / np.sqrt(D) / s_d[:, None]]
    wf_ = [pack_group(w) for w in n((G, D, M)) / np.sqrt(D) / s_d[:, None]]
    wo_ = [pack_group(w) for w in n((G, D, M)) / np.sqrt(D) / s_d[:, None]]
    wc_ = [pack_group(w) for w in n((G, D, M)) / np.sqrt(D) / s_d[:, None]]
    return {
        "h": (n((G, D, N)) * s_d[:, None]).astype(np.float32),
        "wi_words": np.stack([w[0] for w in wi_]),
        "wi_scales": np.stack([w[1] for w in wi_]),
        "wf_words": np.stack([w[0] for w in wf_]),
        "wf_scales": np.stack([w[1] for w in wf_]),
        "wo_words": np.stack([w[0] for w in wo_]),
        "wo_scales": np.stack([w[1] for w in wo_]),
        "wc_words": np.stack([w[0] for w in wc_]),
        "wc_scales": np.stack([w[1] for w in wc_]),
        "xi": (n((G, M, N))).astype(np.float32),
        "xf": (n((G, M, N))).astype(np.float32),
        "xo": (n((G, M, N))).astype(np.float32),
        "xc": (n((G, M, N))).astype(np.float32),
        "c": (n((G, M, N))).astype(np.float32),
    }


def reference(h, wi_words, wi_scales, wf_words, wf_scales, wo_words, wo_scales, wc_words, wc_scales, xi, xf, xo, xc, c):
    wi = np.stack([unpack_group(wi_words[g], wi_scales[g]) for g in range(G)])
    hq = mxq(f64(h), 1, "e4m3")
    zi = wi.transpose(0, 2, 1) @ hq
    wf = np.stack([unpack_group(wf_words[g], wf_scales[g]) for g in range(G)])
    zf = wf.transpose(0, 2, 1) @ hq
    wo = np.stack([unpack_group(wo_words[g], wo_scales[g]) for g in range(G)])
    zo = wo.transpose(0, 2, 1) @ hq
    wc = np.stack([unpack_group(wc_words[g], wc_scales[g]) for g in range(G)])
    zc = wc.transpose(0, 2, 1) @ hq
    cn = sigmoid(zf + f64(xf)) * f64(c) + sigmoid(zi + f64(xi)) * np.tanh(zc + f64(xc))
    y = sigmoid(zo + f64(xo)) * np.tanh(cn)
    return y

@@ -1,0 +1,198 @@
+from contextlib import ExitStack
+
+import concourse.mybir as mybir
+
+G, D, M, N = 4, 128, 128, 512
+FLOPS = 2 * 4 * G * D * M * N
+
+F32 = mybir.dt.float32
+BF16 = mybir.dt.bfloat16
+I32 = mybir.dt.int32
+U32 = mybir.dt.uint32
+U8 = mybir.dt.uint8
+FP8X4 = mybir.dt.float8_e4m3fn_x4
+FP4X4 = mybir.dt.float4_e2m1fn_x4
+ACT = mybir.ActivationFunctionType
+ALU = mybir.AluOpType
+
+GATES = ["i", "c", "f", "o"]
+P = 128
+PACK = 4
+ROWS = D // PACK
+HALF = N // 2
+SCALAR_COLS = 192
+
+
+def tile_rows_cell_lstm_kernel(
+    tc, h, wi_words, wi_scales, wf_words, wf_scales, wo_words, wo_scales, wc_words, wc_scales,
+    xi, xf, xo, xc, c, out,
+):
+    nc = tc.nc
+    words_in = {"i": wi_words, "c": wc_words, "f": wf_words, "o": wo_words}
+    scales_in = {"i": wi_scales, "c": wc_scales, "f": wf_scales, "o": wo_scales}
+    x_in = {"i": xi, "c": xc, "f": xf, "o": xo, "cell": c}
+    func = {"i": ACT.Sigmoid, "c": ACT.Tanh, "f": ACT.Sigmoid, "o": ACT.Sigmoid}
+    bank_of = {"i": 0, "c": 1, "f": 0, "o": 1}
+
+    with ExitStack() as ctx:
+        sb = ctx.enter_context(tc.tile_pool(name="sb", bufs=1))
+        ps = ctx.enter_context(tc.psum_pool(name="ps", bufs=1))
+        ctx.enter_context(tc.manual_schedule())
+
+        h_raw = sb.tile([P, PACK, N], F32, name="h_raw")
+        h_bf = sb.tile([P, N, PACK], BF16, name="h_bf", align_bytes=64)
+        h_codes = sb.tile([P, N], U32, name="h_codes", align_bytes=64)
+        h_scales = sb.tile([P, N], U8, name="h_scales", align_bytes=64)
+        words = {k: sb.tile([P, 2 * M], U8, name="words_" + k, align_bytes=64) for k in "icfo"}
+        staged = sb.tile([ROWS, 4, G, M], U8, name="staged", align_bytes=64)
+        placed = sb.tile([P, 4, M], U8, name="placed", align_bytes=64)
+        x = {
+            (g, k): sb.tile([P, N], F32, name="x_%s_%d" % (k, g))
+            for g in range(G) for k in x_in
+        }
+        new_cell = sb.tile([P, N], F32, name="new_cell")
+        last_cell = sb.tile([P, N], F32, name="last_cell")
+        warm = sb.tile([P, 8], F32, name="warm")
+        banks = {
+            (g, b): ps.tile([P, N], F32, name="bank_%d_%d" % (g, b))
+            for g in range(G) for b in range(2)
+        }
+
+        def load_words(queue, k):
+            queue.dma_start(
+                out=words[k][:].bitcast(I32),
+                in_=words_in[k].rearrange("g p b -> (g p) b").bitcast(I32),
+            )
+
+        def load_scales(queue, k):
+            queue.dma_start(
+                out=staged[0:4, GATES.index(k), :, :].bitcast(I32),
+                in_=scales_in[k].bitcast(I32).rearrange("g t m -> t g m"),
+            )
+
+        def weight_scales(g, k):
+            if g == 0:
+                return staged[:, GATES.index(k), 0, :]
+            return placed[ROWS * g : ROWS * (g + 1), GATES.index(k), :]
+
+        def load_x(g, k):
+            nc.sync.dma_start(out=x[g, k][:], in_=x_in[k][g])
+
+        nc.sync.dma_start(out=h_raw[:], in_=h.rearrange("g (p j) n -> (g p) j n", j=PACK))
+        nc.vector.memset(staged[:].rearrange("p k g m -> p (k g m)").bitcast(I32), 0)
+        for k in "ic":
+            load_words(nc.sync, k)
+        for k in "ic":
+            load_scales(nc.sync, k)
+        for k in "fo":
+            load_scales(nc.gpsimd, k)
+        for k in "fo":
+            load_words(nc.gpsimd, k)
+        for g in range(1, G):
+            nc.gpsimd.dma_start(
+                out=placed[ROWS * g : ROWS * (g + 1), :, :].bitcast(I32),
+                in_=staged[:, :, g, :].bitcast(I32),
+            )
+        for g in range(G):
+            for k in ("i", "c", "f", "cell", "o"):
+                load_x(g, k)
+
+        nc.vector.memset(warm[:], 0.0)
+        nc.scalar.activation(out=warm[:], in_=warm[:], func=ACT.Sigmoid)
+
+        def interleave(copy, a, b):
+            copy(
+                out=h_bf[:, a:b, :].rearrange("p (c i) j -> p c j i", i=4),
+                in_=h_raw[:, :, a:b].rearrange("p j (c i) -> p c j i", i=4),
+            )
+
+        def quantize(a, b):
+            nc.vector.quantize_mx(
+                out=h_codes[:, a:b].bitcast(FP8X4),
+                scales=h_scales[:, a:b],
+                in_=h_bf[:, a:b, :].rearrange("p n j -> p (n j)"),
+            )
+
+        interleave(nc.vector.tensor_copy, 0, HALF)
+        interleave(nc.scalar.copy, N - SCALAR_COLS, N)
+        interleave(nc.vector.tensor_copy, HALF, N - SCALAR_COLS)
+        quantize(0, HALF)
+        quantize(HALF, N)
+
+        def product(g, k):
+            rows = slice(ROWS * g, ROWS * (g + 1))
+            nc.tensor.matmul_mx(
+                out=banks[g, bank_of[k]][:],
+                lhsT=words[k][rows, :].bitcast(FP4X4),
+                lhsT_scale=weight_scales(g, k),
+                rhs=h_codes[rows, :].bitcast(FP8X4),
+                rhs_scale=h_scales[rows, :],
+                start=True,
+                stop=True,
+            )
+
+        def add_sum(g, k):
+            nc.vector.tensor_tensor(
+                out=x[g, k][:], in0=banks[g, bank_of[k]][:], in1=x[g, k][:], op=ALU.add
+            )
+            if k in "ic":
+                product(g, "f" if k == "i" else "o")
+                if g + 1 < G:
+                    product(g + 1, k)
+
+        def activate(g, k):
+            nc.scalar.activation(out=x[g, k][:], in_=x[g, k][:], func=func[k])
+
+        def gate(g, k):
+            add_sum(g, k)
+            activate(g, k)
+
+        def mul(engine, g, a, b):
+            engine.tensor_tensor(out=x[g, a][:], in0=x[g, a][:], in1=x[g, b][:], op=ALU.mult)
+
+        def cell_sum(engine, g, cell, cols):
+            engine.tensor_tensor(
+                out=cell[:, cols], in0=x[g, "i"][:, cols], in1=x[g, "f"][:, cols], op=ALU.add
+            )
+
+        def cell_tanh(cell, cols):
+            nc.scalar.activation(out=cell[:, cols], in_=cell[:, cols], func=ACT.Tanh)
+
+        def finish(g, cell, cols):
+            nc.vector.tensor_tensor(
+                out=x[g, "o"][:, cols], in0=x[g, "o"][:, cols], in1=cell[:, cols], op=ALU.mult
+            )
+            nc.sync.dma_start(out=out[g, :, cols], in_=x[g, "o"][:, cols])
+
+        whole = slice(0, N)
+        product(0, "i")
+        product(0, "c")
+        gate(0, "i")
+        for g in range(G - 1):
+            gate(g, "c")
+            gate(g, "f")
+            if g > 0:
+                cell_sum(nc.gpsimd, g - 1, new_cell, whole)
+                cell_tanh(new_cell, whole)
+            mul(nc.vector, g, "i", "c")
+            mul(nc.gpsimd, g, "f", "cell")
+            gate(g, "o")
+            gate(g + 1, "i")
+            if g > 0:
+                finish(g - 1, new_cell, whole)
+
+        g = G - 1
+        gate(g, "c")
+        gate(g, "f")
+        cell_sum(nc.gpsimd, g - 1, new_cell, whole)
+        cell_tanh(new_cell, whole)
+        mul(nc.vector, g, "i", "c")
+        mul(nc.vector, g, "f", "cell")
+        gate(g, "o")
+        halves = (slice(0, HALF), slice(HALF, N))
+        for cols in halves:
+            cell_sum(nc.vector, g, last_cell, cols)
+            cell_tanh(last_cell, cols)
+        finish(g - 1, new_cell, whole)
+        for cols in halves:
+            finish(g, last_cell, cols)

@@ -21,6 +21,7 @@ PACK = 4
 ROWS = D // PACK
 HALF = N // 2
 SCALAR_COLS = 192
+POOL_COLS = [512,768,864,384]
 
 
 def tile_rows_cell_lstm_kernel(
@@ -43,20 +44,23 @@ def tile_rows_cell_lstm_kernel(
         h_bf = sb.tile([P, N, PACK], BF16, name="h_bf", align_bytes=64)
         h_codes = sb.tile([P, N], U32, name="h_codes", align_bytes=64)
         h_scales = sb.tile([P, N], U8, name="h_scales", align_bytes=64)
-        words = {k: sb.tile([P, 2 * M], U8, name="words_" + k, align_bytes=64) for k in "icfo"}
+        words = {k: sb.tile([P, 2 * M], U8, name="words_" + k, align_bytes=64) for k in GATES}
         staged = sb.tile([ROWS, 4, G, M], U8, name="staged", align_bytes=64)
         placed = sb.tile([P, 4, M], U8, name="placed", align_bytes=64)
-        x = {
-            (g, k): sb.tile([P, N], F32, name="x_%s_%d" % (k, g))
-            for g in range(G) for k in x_in
-        }
-        new_cell = sb.tile([P, N], F32, name="new_cell")
-        last_cell = sb.tile([P, N], F32, name="last_cell")
+        left = sb.tile([P, G, 2, N], F32, name="left")
+        right = sb.tile([P, G, 2, N], F32, name="right")
+        outs = sb.tile([P, G, N], F32, name="outs")
+        work = [sb.tile([P, 2 * N], F32, name="work_%d" % b) for b in range(3)]
         warm = sb.tile([P, 8], F32, name="warm")
         banks = {
             (g, b): ps.tile([P, N], F32, name="bank_%d_%d" % (g, b))
             for g in range(G) for b in range(2)
         }
+
+        def x(g, k):
+            if k == "o":
+                return outs[:, g, :]
+            return (left if k in ("i", "f") else right)[:, g, 0 if k in ("i", "c") else 1, :]
 
         def load_words(queue, k):
             queue.dma_start(
@@ -64,10 +68,16 @@ def tile_rows_cell_lstm_kernel(
                 in_=words_in[k].rearrange("g p b -> (g p) b").bitcast(I32),
             )
 
-        def load_scales(queue, k):
-            queue.dma_start(
+        def load_scales(k):
+            nc.sync.dma_start(
                 out=staged[0:4, GATES.index(k), :, :].bitcast(I32),
                 in_=scales_in[k].bitcast(I32).rearrange("g t m -> t g m"),
+            )
+
+        def place_scales(g):
+            nc.sync.dma_start(
+                out=placed[ROWS * g : ROWS * (g + 1), :, :].bitcast(I32),
+                in_=staged[:, :, g, :].bitcast(I32),
             )
 
         def weight_scales(g, k):
@@ -76,26 +86,38 @@ def tile_rows_cell_lstm_kernel(
             return placed[ROWS * g : ROWS * (g + 1), GATES.index(k), :]
 
         def load_x(g, k):
-            nc.sync.dma_start(out=x[g, k][:], in_=x_in[k][g])
+            nc.sync.dma_start(out=x(g, k), in_=x_in[k][g])
 
-        nc.sync.dma_start(out=h_raw[:], in_=h.rearrange("g (p j) n -> (g p) j n", j=PACK))
-        nc.vector.memset(staged[:].rearrange("p k g m -> p (k g m)").bitcast(I32), 0)
-        for k in "ic":
-            load_words(nc.sync, k)
-        for k in "ic":
-            load_scales(nc.sync, k)
-        for k in "fo":
-            load_scales(nc.gpsimd, k)
-        for k in "fo":
-            load_words(nc.gpsimd, k)
-        for g in range(1, G):
-            nc.gpsimd.dma_start(
-                out=placed[ROWS * g : ROWS * (g + 1), :, :].bitcast(I32),
-                in_=staged[:, :, g, :].bitcast(I32),
+        def load_x_pair(k):
+            nc.sync.dma_start(
+                out=x(slice(0, 2), k), in_=x_in[k][0:2].rearrange("g m n -> m g n")
             )
-        for g in range(G):
-            for k in ("i", "c", "f", "cell", "o"):
+
+        nc.vector.memset(staged[:].rearrange("p k g m -> p (k g m)").bitcast(I32), 0)
+        load_words(nc.scalar, "i")
+        load_words(nc.scalar, "c")
+        nc.sync.dma_start(out=h_raw[:], in_=h.rearrange("g (p j) n -> (g p) j n", j=PACK))
+        for k in GATES:
+            load_scales(k)
+        load_x_pair("i")
+        load_x_pair("c")
+        load_words(nc.sync, "f")
+        place_scales(1)
+        load_x(0, "f")
+        load_x(0, "cell")
+        load_x(1, "f")
+        load_words(nc.sync, "o")
+        place_scales(2)
+        load_x(1, "cell")
+        for g in range(2, G):
+            load_x(g, "i")
+            load_x(g - 2, "o")
+            if g + 1 < G:
+                place_scales(g + 1)
+            for k in ("c", "f", "cell"):
                 load_x(g, k)
+        load_x(2, "o")
+        load_x(3, "o")
 
         nc.vector.memset(warm[:], 0.0)
         nc.scalar.activation(out=warm[:], in_=warm[:], func=ACT.Sigmoid)
@@ -131,68 +153,88 @@ def tile_rows_cell_lstm_kernel(
                 stop=True,
             )
 
-        def add_sum(g, k):
-            nc.vector.tensor_tensor(
-                out=x[g, k][:], in0=banks[g, bank_of[k]][:], in1=x[g, k][:], op=ALU.add
-            )
-            if k in "ic":
-                product(g, "f" if k == "i" else "o")
-                if g + 1 < G:
-                    product(g + 1, k)
-
-        def activate(g, k):
-            nc.scalar.activation(out=x[g, k][:], in_=x[g, k][:], func=func[k])
-
         def gate(g, k):
-            add_sum(g, k)
-            activate(g, k)
-
-        def mul(engine, g, a, b):
-            engine.tensor_tensor(out=x[g, a][:], in0=x[g, a][:], in1=x[g, b][:], op=ALU.mult)
-
-        def cell_sum(engine, g, cell, cols):
-            engine.tensor_tensor(
-                out=cell[:, cols], in0=x[g, "i"][:, cols], in1=x[g, "f"][:, cols], op=ALU.add
-            )
-
-        def cell_tanh(cell, cols):
-            nc.scalar.activation(out=cell[:, cols], in_=cell[:, cols], func=ACT.Tanh)
-
-        def finish(g, cell, cols):
             nc.vector.tensor_tensor(
-                out=x[g, "o"][:, cols], in0=x[g, "o"][:, cols], in1=cell[:, cols], op=ALU.mult
+                out=x(g, k), in0=banks[g, bank_of[k]][:], in1=x(g, k), op=ALU.add
             )
-            nc.sync.dma_start(out=out[g, :, cols], in_=x[g, "o"][:, cols])
+            nc.scalar.activation(out=x(g, k), in_=x(g, k), func=func[k])
 
-        whole = slice(0, N)
-        product(0, "i")
-        product(0, "c")
-        gate(0, "i")
-        for g in range(G - 1):
+        def products(engine, g, dst, a, b):
+            if a == b:
+                return
+            engine.tensor_tensor(
+                out=dst[:, a:b],
+                in0=left[:, g].rearrange("p u n -> p (u n)")[:, a:b],
+                in1=right[:, g].rearrange("p u n -> p (u n)")[:, a:b],
+                op=ALU.mult,
+            )
+
+        def cell_sum(src, dst, a=0, b=N):
+            nc.vector.tensor_tensor(
+                out=dst[:, a:b], in0=src[:, a:b], in1=src[:, N + a : N + b], op=ALU.add
+            )
+            nc.scalar.activation(out=dst[:, a:b], in_=dst[:, a:b], func=ACT.Tanh)
+
+        def finish(g, cell, a=0, b=N):
+            nc.vector.tensor_tensor(
+                out=outs[:, g, a:b], in0=outs[:, g, a:b], in1=cell[:, a:b], op=ALU.mult
+            )
+            nc.sync.dma_start(out=out[g, :, a:b], in_=outs[:, g, a:b])
+
+        def window(g):
+            product(g - 2, "o")
+            product(g, "c")
+            gate(g, "i")
+            product(g, "f")
+            if g + 1 < G:
+                product(g + 1, "i")
+            gate(g - 2, "o")
             gate(g, "c")
             gate(g, "f")
-            if g > 0:
-                cell_sum(nc.gpsimd, g - 1, new_cell, whole)
-                cell_tanh(new_cell, whole)
-            mul(nc.vector, g, "i", "c")
-            mul(nc.gpsimd, g, "f", "cell")
-            gate(g, "o")
-            gate(g + 1, "i")
-            if g > 0:
-                finish(g - 1, new_cell, whole)
 
-        g = G - 1
-        gate(g, "c")
-        gate(g, "f")
-        cell_sum(nc.gpsimd, g - 1, new_cell, whole)
-        cell_tanh(new_cell, whole)
-        mul(nc.vector, g, "i", "c")
-        mul(nc.vector, g, "f", "cell")
-        gate(g, "o")
-        halves = (slice(0, HALF), slice(HALF, N))
-        for cols in halves:
-            cell_sum(nc.vector, g, last_cell, cols)
-            cell_tanh(last_cell, cols)
-        finish(g - 1, new_cell, whole)
-        for cols in halves:
-            finish(g, last_cell, cols)
+        wa, wb, wc = work
+        cell0 = wc[:, 0:N]
+        cell1 = wc[:, N : 2 * N]
+
+        product(0, "i")
+        product(0, "c")
+        product(1, "i")
+        gate(0, "i")
+        product(0, "f")
+        product(1, "c")
+        gate(0, "c")
+        products(nc.gpsimd, 0, wa, 0, POOL_COLS[0])
+        gate(1, "i")
+        product(1, "f")
+        product(2, "i")
+        gate(0, "f")
+        gate(1, "c")
+        gate(1, "f")
+        products(nc.vector, 0, wa, POOL_COLS[0], 2 * N)
+
+        products(nc.gpsimd, 1, wb, 0, POOL_COLS[1])
+        window(2)
+        products(nc.vector, 1, wb, POOL_COLS[1], 2 * N)
+        cell_sum(wa, cell0)
+        cell_sum(wb, cell1)
+
+        products(nc.gpsimd, 2, wa, 0, POOL_COLS[2])
+        window(3)
+        products(nc.vector, 2, wa, POOL_COLS[2], 2 * N)
+        finish(0, cell0)
+        finish(1, cell1)
+        cell_sum(wa, wa)
+
+        products(nc.gpsimd, 3, wc, 0, POOL_COLS[3])
+        product(2, "o")
+        product(3, "o")
+        gate(2, "o")
+        gate(3, "o")
+        products(nc.vector, 3, wc, N, N + HALF)
+        products(nc.vector, 3, wc, POOL_COLS[3], N)
+        products(nc.vector, 3, wc, N + HALF, 2 * N)
+        cell_sum(wc, wc, 0, HALF)
+        cell_sum(wc, wc, HALF, N)
+        finish(2, wa)
+        finish(3, wc, 0, HALF)
+        finish(3, wc, HALF, N)

@@ -21,7 +21,7 @@ PACK = 4
 ROWS = D // PACK
 HALF = N // 2
 SCALAR_COLS = 192
-POOL_COLS = [512,768,864,384]
+POOL_COLS = [512,1024,656,384]
 
 
 def tile_rows_cell_lstm_kernel(
@@ -50,7 +50,8 @@ def tile_rows_cell_lstm_kernel(
         left = sb.tile([P, G, 2, N], F32, name="left")
         right = sb.tile([P, G, 2, N], F32, name="right")
         outs = sb.tile([P, G, N], F32, name="outs")
-        work = [sb.tile([P, 2 * N], F32, name="work_%d" % b) for b in range(3)]
+        prods = sb.tile([P, 4 * N], F32, name="prods")
+        wc = sb.tile([P, 2 * N], F32, name="cells")
         warm = sb.tile([P, 8], F32, name="warm")
         banks = {
             (g, b): ps.tile([P, N], F32, name="bank_%d_%d" % (g, b))
@@ -94,30 +95,35 @@ def tile_rows_cell_lstm_kernel(
             )
 
         nc.vector.memset(staged[:].rearrange("p k g m -> p (k g m)").bitcast(I32), 0)
-        load_words(nc.scalar, "i")
-        load_words(nc.scalar, "c")
+        load_words(nc.sync, "i")
         nc.sync.dma_start(out=h_raw[:], in_=h.rearrange("g (p j) n -> (g p) j n", j=PACK))
+        load_words(nc.sync, "c")
         for k in GATES:
             load_scales(k)
         load_x_pair("i")
-        load_x_pair("c")
-        load_words(nc.sync, "f")
+        load_x(0, "c")
         place_scales(1)
+        load_words(nc.sync, "f")
+        load_x(1, "c")
         load_x(0, "f")
-        load_x(0, "cell")
-        load_x(1, "f")
-        load_words(nc.sync, "o")
         place_scales(2)
+        load_x(2, "i")
+        load_x(0, "cell")
+        load_words(nc.sync, "o")
+        load_x(1, "f")
+        place_scales(3)
+        load_x(2, "c")
+        load_x(0, "o")
+        load_x(2, "f")
+        load_x(3, "i")
         load_x(1, "cell")
-        for g in range(2, G):
-            load_x(g, "i")
-            load_x(g - 2, "o")
-            if g + 1 < G:
-                place_scales(g + 1)
-            for k in ("c", "f", "cell"):
-                load_x(g, k)
+        load_x(2, "cell")
+        load_x(1, "o")
+        load_x(3, "c")
+        load_x(3, "f")
         load_x(2, "o")
         load_x(3, "o")
+        load_x(3, "cell")
 
         nc.vector.memset(warm[:], 0.0)
         nc.scalar.activation(out=warm[:], in_=warm[:], func=ACT.Sigmoid)
@@ -164,8 +170,8 @@ def tile_rows_cell_lstm_kernel(
                 return
             engine.tensor_tensor(
                 out=dst[:, a:b],
-                in0=left[:, g].rearrange("p u n -> p (u n)")[:, a:b],
-                in1=right[:, g].rearrange("p u n -> p (u n)")[:, a:b],
+                in0=left[:, g:].rearrange("p g u n -> p (g u n)")[:, a:b],
+                in1=right[:, g:].rearrange("p g u n -> p (g u n)")[:, a:b],
                 op=ALU.mult,
             )
 
@@ -181,53 +187,54 @@ def tile_rows_cell_lstm_kernel(
             )
             nc.sync.dma_start(out=out[g, :, a:b], in_=outs[:, g, a:b])
 
-        def window(g):
-            product(g - 2, "o")
-            product(g, "c")
-            gate(g, "i")
-            product(g, "f")
-            if g + 1 < G:
-                product(g + 1, "i")
-            gate(g - 2, "o")
-            gate(g, "c")
-            gate(g, "f")
-
-        wa, wb, wc = work
+        wa = prods[:, 0 : 2 * N]
+        wb = prods[:, 2 * N : 4 * N]
         cell0 = wc[:, 0:N]
         cell1 = wc[:, N : 2 * N]
 
         product(0, "i")
         product(0, "c")
         product(1, "i")
+        product(1, "c")
         gate(0, "i")
         product(0, "f")
-        product(1, "c")
+        product(2, "i")
         gate(0, "c")
-        products(nc.gpsimd, 0, wa, 0, POOL_COLS[0])
+        products(nc.gpsimd, 0, prods, 0, N)
         gate(1, "i")
         product(1, "f")
-        product(2, "i")
-        gate(0, "f")
         gate(1, "c")
+        gate(0, "f")
+        products(nc.gpsimd, 0, prods, N, N + POOL_COLS[1])
+        product(2, "c")
+        product(0, "o")
+        gate(2, "i")
+        product(2, "f")
+        product(3, "i")
         gate(1, "f")
-        products(nc.vector, 0, wa, POOL_COLS[0], 2 * N)
-
-        products(nc.gpsimd, 1, wb, 0, POOL_COLS[1])
-        window(2)
-        products(nc.vector, 1, wb, POOL_COLS[1], 2 * N)
+        gate(2, "c")
+        gate(0, "o")
+        gate(2, "f")
+        product(1, "o")
+        product(3, "c")
+        gate(3, "i")
+        product(3, "f")
+        product(2, "o")
+        products(nc.vector, 0, prods, N + POOL_COLS[1], 4 * N)
         cell_sum(wa, cell0)
         cell_sum(wb, cell1)
 
         products(nc.gpsimd, 2, wa, 0, POOL_COLS[2])
-        window(3)
+        gate(1, "o")
+        gate(3, "c")
+        product(3, "o")
+        gate(3, "f")
         products(nc.vector, 2, wa, POOL_COLS[2], 2 * N)
         finish(0, cell0)
         finish(1, cell1)
         cell_sum(wa, wa)
 
         products(nc.gpsimd, 3, wc, 0, POOL_COLS[3])
-        product(2, "o")
-        product(3, "o")
         gate(2, "o")
         gate(3, "o")
         products(nc.vector, 3, wc, N, N + HALF)

@@ -19,9 +19,12 @@ GATES = ["i", "c", "f", "o"]
 P = 128
 PACK = 4
 ROWS = D // PACK
+BLOCKS = D // 32
+LINE = 4
 HALF = N // 2
 SCALAR_COLS = 192
-POOL_COLS = [512,1024,656,384]
+GPSIMD_COLS_HEAD_2 = 656
+GPSIMD_COLS_HEAD_3 = 384
 
 
 def tile_rows_cell_lstm_kernel(
@@ -45,14 +48,13 @@ def tile_rows_cell_lstm_kernel(
         h_codes = sb.tile([P, N], U32, name="h_codes", align_bytes=64)
         h_scales = sb.tile([P, N], U8, name="h_scales", align_bytes=64)
         words = {k: sb.tile([P, 2 * M], U8, name="words_" + k, align_bytes=64) for k in GATES}
-        staged = sb.tile([ROWS, 4, G, M], U8, name="staged", align_bytes=64)
-        placed = sb.tile([P, 4, M], U8, name="placed", align_bytes=64)
+        staged = sb.tile([ROWS, len(GATES), G, M], U8, name="staged", align_bytes=64)
+        placed = sb.tile([P, len(GATES), M], U8, name="placed", align_bytes=64)
         left = sb.tile([P, G, 2, N], F32, name="left")
         right = sb.tile([P, G, 2, N], F32, name="right")
         outs = sb.tile([P, G, N], F32, name="outs")
         prods = sb.tile([P, 4 * N], F32, name="prods")
-        wc = sb.tile([P, 2 * N], F32, name="cells")
-        warm = sb.tile([P, 8], F32, name="warm")
+        cells = sb.tile([P, 2 * N], F32, name="cells")
         banks = {
             (g, b): ps.tile([P, N], F32, name="bank_%d_%d" % (g, b))
             for g in range(G) for b in range(2)
@@ -63,15 +65,15 @@ def tile_rows_cell_lstm_kernel(
                 return outs[:, g, :]
             return (left if k in ("i", "f") else right)[:, g, 0 if k in ("i", "c") else 1, :]
 
-        def load_words(queue, k):
-            queue.dma_start(
+        def load_words(k):
+            nc.sync.dma_start(
                 out=words[k][:].bitcast(I32),
                 in_=words_in[k].rearrange("g p b -> (g p) b").bitcast(I32),
             )
 
         def load_scales(k):
             nc.sync.dma_start(
-                out=staged[0:4, GATES.index(k), :, :].bitcast(I32),
+                out=staged[0:BLOCKS, GATES.index(k), :, :].bitcast(I32),
                 in_=scales_in[k].bitcast(I32).rearrange("g t m -> t g m"),
             )
 
@@ -89,27 +91,27 @@ def tile_rows_cell_lstm_kernel(
         def load_x(g, k):
             nc.sync.dma_start(out=x(g, k), in_=x_in[k][g])
 
-        def load_x_pair(k):
+        def load_x_heads_0_1(k):
             nc.sync.dma_start(
                 out=x(slice(0, 2), k), in_=x_in[k][0:2].rearrange("g m n -> m g n")
             )
 
         nc.vector.memset(staged[:].rearrange("p k g m -> p (k g m)").bitcast(I32), 0)
-        load_words(nc.sync, "i")
+
+        load_words("i")
         nc.sync.dma_start(out=h_raw[:], in_=h.rearrange("g (p j) n -> (g p) j n", j=PACK))
-        load_words(nc.sync, "c")
+        load_words("c")
         for k in GATES:
             load_scales(k)
-        load_x_pair("i")
-        load_x(0, "c")
+        load_x_heads_0_1("i")
+        load_x_heads_0_1("c")
         place_scales(1)
-        load_words(nc.sync, "f")
-        load_x(1, "c")
+        load_words("f")
         load_x(0, "f")
         place_scales(2)
         load_x(2, "i")
         load_x(0, "cell")
-        load_words(nc.sync, "o")
+        load_words("o")
         load_x(1, "f")
         place_scales(3)
         load_x(2, "c")
@@ -125,13 +127,10 @@ def tile_rows_cell_lstm_kernel(
         load_x(3, "o")
         load_x(3, "cell")
 
-        nc.vector.memset(warm[:], 0.0)
-        nc.scalar.activation(out=warm[:], in_=warm[:], func=ACT.Sigmoid)
-
         def interleave(copy, a, b):
             copy(
-                out=h_bf[:, a:b, :].rearrange("p (c i) j -> p c j i", i=4),
-                in_=h_raw[:, :, a:b].rearrange("p j (c i) -> p c j i", i=4),
+                out=h_bf[:, a:b, :].rearrange("p (c i) j -> p c j i", i=LINE),
+                in_=h_raw[:, :, a:b].rearrange("p j (c i) -> p c j i", i=LINE),
             )
 
         def quantize(a, b):
@@ -147,7 +146,7 @@ def tile_rows_cell_lstm_kernel(
         quantize(0, HALF)
         quantize(HALF, N)
 
-        def product(g, k):
+        def matmul(g, k):
             rows = slice(ROWS * g, ROWS * (g + 1))
             nc.tensor.matmul_mx(
                 out=banks[g, bank_of[k]][:],
@@ -165,9 +164,7 @@ def tile_rows_cell_lstm_kernel(
             )
             nc.scalar.activation(out=x(g, k), in_=x(g, k), func=func[k])
 
-        def products(engine, g, dst, a, b):
-            if a == b:
-                return
+        def multiply(engine, g, dst, a, b):
             engine.tensor_tensor(
                 out=dst[:, a:b],
                 in0=left[:, g:].rearrange("p g u n -> p (g u n)")[:, a:b],
@@ -175,7 +172,7 @@ def tile_rows_cell_lstm_kernel(
                 op=ALU.mult,
             )
 
-        def cell_sum(src, dst, a=0, b=N):
+        def cell_tanh(src, dst, a=0, b=N):
             nc.vector.tensor_tensor(
                 out=dst[:, a:b], in0=src[:, a:b], in1=src[:, N + a : N + b], op=ALU.add
             )
@@ -187,61 +184,60 @@ def tile_rows_cell_lstm_kernel(
             )
             nc.sync.dma_start(out=out[g, :, a:b], in_=outs[:, g, a:b])
 
-        wa = prods[:, 0 : 2 * N]
-        wb = prods[:, 2 * N : 4 * N]
-        cell0 = wc[:, 0:N]
-        cell1 = wc[:, N : 2 * N]
+        low = prods[:, 0 : 2 * N]
+        high = prods[:, 2 * N : 4 * N]
 
-        product(0, "i")
-        product(0, "c")
-        product(1, "i")
-        product(1, "c")
+        matmul(0, "i")
+        matmul(0, "c")
+        matmul(1, "i")
+        matmul(1, "c")
         gate(0, "i")
-        product(0, "f")
-        product(2, "i")
+        matmul(0, "f")
+        matmul(2, "i")
         gate(0, "c")
-        products(nc.gpsimd, 0, prods, 0, N)
+        multiply(nc.gpsimd, 0, prods, 0, N)
         gate(1, "i")
-        product(1, "f")
+        matmul(1, "f")
         gate(1, "c")
         gate(0, "f")
-        products(nc.gpsimd, 0, prods, N, N + POOL_COLS[1])
-        product(2, "c")
-        product(0, "o")
+        multiply(nc.gpsimd, 0, prods, N, 3 * N)
+        matmul(2, "c")
+        matmul(0, "o")
         gate(2, "i")
-        product(2, "f")
-        product(3, "i")
+        matmul(2, "f")
+        matmul(3, "i")
         gate(1, "f")
         gate(2, "c")
         gate(0, "o")
         gate(2, "f")
-        product(1, "o")
-        product(3, "c")
+        matmul(1, "o")
+        matmul(3, "c")
         gate(3, "i")
-        product(3, "f")
-        product(2, "o")
-        products(nc.vector, 0, prods, N + POOL_COLS[1], 4 * N)
-        cell_sum(wa, cell0)
-        cell_sum(wb, cell1)
+        matmul(3, "f")
+        matmul(2, "o")
+        multiply(nc.vector, 0, prods, 3 * N, 4 * N)
+        cell_tanh(low, cells[:, 0:N])
+        cell_tanh(high, cells[:, N : 2 * N])
 
-        products(nc.gpsimd, 2, wa, 0, POOL_COLS[2])
+        multiply(nc.gpsimd, 2, low, 0, GPSIMD_COLS_HEAD_2)
         gate(1, "o")
         gate(3, "c")
-        product(3, "o")
+        matmul(3, "o")
         gate(3, "f")
-        products(nc.vector, 2, wa, POOL_COLS[2], 2 * N)
-        finish(0, cell0)
-        finish(1, cell1)
-        cell_sum(wa, wa)
+        multiply(nc.vector, 2, low, GPSIMD_COLS_HEAD_2, 2 * N)
+        finish(0, cells[:, 0:N])
+        finish(1, cells[:, N : 2 * N])
+        cell_tanh(low, low)
 
-        products(nc.gpsimd, 3, wc, 0, POOL_COLS[3])
+        multiply(nc.gpsimd, 3, cells, 0, GPSIMD_COLS_HEAD_3)
         gate(2, "o")
         gate(3, "o")
-        products(nc.vector, 3, wc, N, N + HALF)
-        products(nc.vector, 3, wc, POOL_COLS[3], N)
-        products(nc.vector, 3, wc, N + HALF, 2 * N)
-        cell_sum(wc, wc, 0, HALF)
-        cell_sum(wc, wc, HALF, N)
-        finish(2, wa)
-        finish(3, wc, 0, HALF)
-        finish(3, wc, HALF, N)
+
+        multiply(nc.vector, 3, cells, N, N + HALF)
+        multiply(nc.vector, 3, cells, GPSIMD_COLS_HEAD_3, N)
+        multiply(nc.vector, 3, cells, N + HALF, 2 * N)
+        cell_tanh(cells, cells, 0, HALF)
+        cell_tanh(cells, cells, HALF, N)
+        finish(2, low)
+        finish(3, cells, 0, HALF)
+        finish(3, cells, HALF, N)

from contextlib import ExitStack

import concourse.mybir as mybir

G, D, M, N = 4, 128, 128, 512
FLOPS = 2 * 4 * G * D * M * N

F32 = mybir.dt.float32
BF16 = mybir.dt.bfloat16
I32 = mybir.dt.int32
U32 = mybir.dt.uint32
U8 = mybir.dt.uint8
FP8X4 = mybir.dt.float8_e4m3fn_x4
FP4X4 = mybir.dt.float4_e2m1fn_x4
ACT = mybir.ActivationFunctionType
ALU = mybir.AluOpType

GATES = ["i", "c", "f", "o"]
P = 128
PACK = 4
ROWS = D // PACK
BLOCKS = D // 32
LINE = 4
HALF = N // 2
SCALAR_COLS = 192
GPSIMD_COLS_HEAD_2 = 656
GPSIMD_COLS_HEAD_3 = 384


def tile_rows_cell_lstm_kernel(
    tc, h, wi_words, wi_scales, wf_words, wf_scales, wo_words, wo_scales, wc_words, wc_scales,
    xi, xf, xo, xc, c, out,
):
    nc = tc.nc
    words_in = {"i": wi_words, "c": wc_words, "f": wf_words, "o": wo_words}
    scales_in = {"i": wi_scales, "c": wc_scales, "f": wf_scales, "o": wo_scales}
    x_in = {"i": xi, "c": xc, "f": xf, "o": xo, "cell": c}
    func = {"i": ACT.Sigmoid, "c": ACT.Tanh, "f": ACT.Sigmoid, "o": ACT.Sigmoid}
    bank_of = {"i": 0, "c": 1, "f": 0, "o": 1}

    with ExitStack() as ctx:
        sb = ctx.enter_context(tc.tile_pool(name="sb", bufs=1))
        ps = ctx.enter_context(tc.psum_pool(name="ps", bufs=1))
        ctx.enter_context(tc.manual_schedule())

        h_raw = sb.tile([P, PACK, N], F32, name="h_raw")
        h_bf = sb.tile([P, N, PACK], BF16, name="h_bf", align_bytes=64)
        h_codes = sb.tile([P, N], U32, name="h_codes", align_bytes=64)
        h_scales = sb.tile([P, N], U8, name="h_scales", align_bytes=64)
        words = {k: sb.tile([P, 2 * M], U8, name="words_" + k, align_bytes=64) for k in GATES}
        staged = sb.tile([ROWS, len(GATES), G, M], U8, name="staged", align_bytes=64)
        placed = sb.tile([P, len(GATES), M], U8, name="placed", align_bytes=64)
        left = sb.tile([P, G, 2, N], F32, name="left")
        right = sb.tile([P, G, 2, N], F32, name="right")
        outs = sb.tile([P, G, N], F32, name="outs")
        prods = sb.tile([P, 4 * N], F32, name="prods")
        cells = sb.tile([P, 2 * N], F32, name="cells")
        banks = {
            (g, b): ps.tile([P, N], F32, name="bank_%d_%d" % (g, b))
            for g in range(G) for b in range(2)
        }

        def x(g, k):
            if k == "o":
                return outs[:, g, :]
            return (left if k in ("i", "f") else right)[:, g, 0 if k in ("i", "c") else 1, :]

        def load_words(k):
            nc.sync.dma_start(
                out=words[k][:].bitcast(I32),
                in_=words_in[k].rearrange("g p b -> (g p) b").bitcast(I32),
            )

        def load_scales(k):
            nc.sync.dma_start(
                out=staged[0:BLOCKS, GATES.index(k), :, :].bitcast(I32),
                in_=scales_in[k].bitcast(I32).rearrange("g t m -> t g m"),
            )

        def place_scales(g):
            nc.sync.dma_start(
                out=placed[ROWS * g : ROWS * (g + 1), :, :].bitcast(I32),
                in_=staged[:, :, g, :].bitcast(I32),
            )

        def weight_scales(g, k):
            if g == 0:
                return staged[:, GATES.index(k), 0, :]
            return placed[ROWS * g : ROWS * (g + 1), GATES.index(k), :]

        def load_x(g, k):
            nc.sync.dma_start(out=x(g, k), in_=x_in[k][g])

        def load_x_heads_0_1(k):
            nc.sync.dma_start(
                out=x(slice(0, 2), k), in_=x_in[k][0:2].rearrange("g m n -> m g n")
            )

        nc.vector.memset(staged[:].rearrange("p k g m -> p (k g m)").bitcast(I32), 0)

        load_words("i")
        nc.sync.dma_start(out=h_raw[:], in_=h.rearrange("g (p j) n -> (g p) j n", j=PACK))
        load_words("c")
        for k in GATES:
            load_scales(k)
        load_x_heads_0_1("i")
        load_x_heads_0_1("c")
        place_scales(1)
        load_words("f")
        load_x(0, "f")
        place_scales(2)
        load_x(2, "i")
        load_x(0, "cell")
        load_words("o")
        load_x(1, "f")
        place_scales(3)
        load_x(2, "c")
        load_x(0, "o")
        load_x(2, "f")
        load_x(3, "i")
        load_x(1, "cell")
        load_x(2, "cell")
        load_x(1, "o")
        load_x(3, "c")
        load_x(3, "f")
        load_x(2, "o")
        load_x(3, "o")
        load_x(3, "cell")

        def interleave(copy, a, b):
            copy(
                out=h_bf[:, a:b, :].rearrange("p (c i) j -> p c j i", i=LINE),
                in_=h_raw[:, :, a:b].rearrange("p j (c i) -> p c j i", i=LINE),
            )

        def quantize(a, b):
            nc.vector.quantize_mx(
                out=h_codes[:, a:b].bitcast(FP8X4),
                scales=h_scales[:, a:b],
                in_=h_bf[:, a:b, :].rearrange("p n j -> p (n j)"),
            )

        interleave(nc.vector.tensor_copy, 0, HALF)
        interleave(nc.scalar.copy, N - SCALAR_COLS, N)
        interleave(nc.vector.tensor_copy, HALF, N - SCALAR_COLS)
        quantize(0, HALF)
        quantize(HALF, N)

        def matmul(g, k):
            rows = slice(ROWS * g, ROWS * (g + 1))
            nc.tensor.matmul_mx(
                out=banks[g, bank_of[k]][:],
                lhsT=words[k][rows, :].bitcast(FP4X4),
                lhsT_scale=weight_scales(g, k),
                rhs=h_codes[rows, :].bitcast(FP8X4),
                rhs_scale=h_scales[rows, :],
                start=True,
                stop=True,
            )

        def gate(g, k):
            nc.vector.tensor_tensor(
                out=x(g, k), in0=banks[g, bank_of[k]][:], in1=x(g, k), op=ALU.add
            )
            nc.scalar.activation(out=x(g, k), in_=x(g, k), func=func[k])

        def multiply(engine, g, dst, a, b):
            engine.tensor_tensor(
                out=dst[:, a:b],
                in0=left[:, g:].rearrange("p g u n -> p (g u n)")[:, a:b],
                in1=right[:, g:].rearrange("p g u n -> p (g u n)")[:, a:b],
                op=ALU.mult,
            )

        def cell_tanh(src, dst, a=0, b=N):
            nc.vector.tensor_tensor(
                out=dst[:, a:b], in0=src[:, a:b], in1=src[:, N + a : N + b], op=ALU.add
            )
            nc.scalar.activation(out=dst[:, a:b], in_=dst[:, a:b], func=ACT.Tanh)

        def finish(g, cell, a=0, b=N):
            nc.vector.tensor_tensor(
                out=outs[:, g, a:b], in0=outs[:, g, a:b], in1=cell[:, a:b], op=ALU.mult
            )
            nc.sync.dma_start(out=out[g, :, a:b], in_=outs[:, g, a:b])

        low = prods[:, 0 : 2 * N]
        high = prods[:, 2 * N : 4 * N]

        matmul(0, "i")
        matmul(0, "c")
        matmul(1, "i")
        matmul(1, "c")
        gate(0, "i")
        matmul(0, "f")
        matmul(2, "i")
        gate(0, "c")
        multiply(nc.gpsimd, 0, prods, 0, N)
        gate(1, "i")
        matmul(1, "f")
        gate(1, "c")
        gate(0, "f")
        multiply(nc.gpsimd, 0, prods, N, 3 * N)
        matmul(2, "c")
        matmul(0, "o")
        gate(2, "i")
        matmul(2, "f")
        matmul(3, "i")
        gate(1, "f")
        gate(2, "c")
        gate(0, "o")
        gate(2, "f")
        matmul(1, "o")
        matmul(3, "c")
        gate(3, "i")
        matmul(3, "f")
        matmul(2, "o")
        multiply(nc.vector, 0, prods, 3 * N, 4 * N)
        cell_tanh(low, cells[:, 0:N])
        cell_tanh(high, cells[:, N : 2 * N])

        multiply(nc.gpsimd, 2, low, 0, GPSIMD_COLS_HEAD_2)
        gate(1, "o")
        gate(3, "c")
        matmul(3, "o")
        gate(3, "f")
        multiply(nc.vector, 2, low, GPSIMD_COLS_HEAD_2, 2 * N)
        finish(0, cells[:, 0:N])
        finish(1, cells[:, N : 2 * N])
        cell_tanh(low, low)

        multiply(nc.gpsimd, 3, cells, 0, GPSIMD_COLS_HEAD_3)
        gate(2, "o")
        gate(3, "o")

        multiply(nc.vector, 3, cells, N, N + HALF)
        multiply(nc.vector, 3, cells, GPSIMD_COLS_HEAD_3, N)
        multiply(nc.vector, 3, cells, N + HALF, 2 * N)
        cell_tanh(cells, cells, 0, HALF)
        cell_tanh(cells, cells, HALF, N)
        finish(2, low)
        finish(3, cells, 0, HALF)
        finish(3, cells, HALF, N)
